import numpy as np
import ml_dtypes


def mxq(x, axis, fmt="e4m3"):
    dtype, down = {"e4m3": (ml_dtypes.float8_e4m3fn, 7), "e5m2": (ml_dtypes.float8_e5m2, 14)}[fmt]
    v = np.moveaxis(np.asarray(x, np.float32).astype(ml_dtypes.bfloat16).astype(np.float64), axis, -1)
    blocks = v.reshape(v.shape[:-1] + (-1, 32))
    amax = np.abs(blocks).max(-1, keepdims=True)
    byte = np.maximum(np.where(amax > 0, np.frexp(amax)[1] - 1 + 127, 0) - down, 1)
    scale = np.exp2(byte - 127.0)
    codes = (blocks / scale).astype(np.float32).astype(dtype).astype(np.float64)
    return np.moveaxis((codes * scale).reshape(v.shape), -1, axis)


WIDE = False


def mx_kscale(k):
    if not WIDE:
        return np.ones(k)
    levels = np.array([10, -10, 5, -5, 0])
    if k % 512:
        return np.exp2(np.random.permutation(np.resize(levels, k // 32))).repeat(32)
    a = np.empty((k // 512, 16))
    for p in range(k // 512):
        a[p, :8] = np.random.permutation(np.resize(levels, 8))
        for g in range(8):
            far = levels[np.abs(levels - a[p, g]) >= 10]
            a[p, g + 8] = far[np.random.randint(len(far))]
    return np.exp2(a.ravel()).repeat(32)


def f64(x):
    return np.asarray(x).astype(np.float64)


def striped(idx):
    return np.tile(idx.reshape(-1, 16).T, (8, 1)).astype(np.uint16)


def unstriped(offs):
    return offs[:16].T.reshape(-1).astype(np.int64)


def relu(v):
    return np.maximum(v, 0.0)


K, T, E, C, H, N = 1024, 512, 4, 256, 512, 256


def by_expert(wq, xq):
    return np.concatenate([wq[e].T @ xq[:, e * C:(e + 1) * C] for e in range(E)], axis=1)


def setup_inputs():
    n = np.random.standard_normal
    s = mx_kscale(K)[:, None]
    u = mx_kscale(H)
    first = np.random.permutation(np.repeat(np.arange(E), T // E))
    second = (first + 1 + np.random.permutation(np.repeat(np.arange(E - 1), -(-T // (E - 1)))[:T])) % E
    while np.bincount(second, minlength=E).max() != T // E:
        load = np.bincount(second, minlength=E); hi, lo = int(load.argmax()), int(load.argmin())
        t = np.flatnonzero((second == hi) & (first != lo))[0]; second[t] = lo
    slot_token = np.empty(E * C, np.int64); pos = np.empty((2, T), np.int64); fill = np.zeros(E, np.int64)
    place = np.stack([np.random.permutation(C) for _ in range(E)])
    for r, deal in enumerate((first, second)):
        for t in np.random.permutation(T):
            e = deal[t]; j = e * C + place[e, fill[e]]; fill[e] += 1; slot_token[j] = t; pos[r, t] = j
    g = np.random.uniform(0.2, 0.8, T)
    return {
        "xT": (n((K, T)) * s).astype(np.float32),
        "w1": (n((E + 1, K, H)) / np.sqrt(K) / s[None]).astype(np.float32),
        "w3": (n((E + 1, K, H)) / np.sqrt(K) / s[None] * u[None, None, :]).astype(np.float32),
        "w2": (n((E + 1, H, N)) / np.sqrt(H) / u[None, :, None]).astype(np.float32),
        "gate": np.stack([np.tile(g, (N, 1)), np.tile(1.0 - g, (N, 1))]).astype(np.float32),
        "offs": striped(slot_token),
        "pos1": striped(pos[0]),
        "pos2": striped(pos[1]),
    }


def reference(xT, w1, w3, w2, gate, offs, pos1, pos2):
    idx = unstriped(offs)
    w1q, w3q, w2q = mxq(f64(w1), 1, "e4m3"), mxq(f64(w3), 1, "e4m3"), mxq(f64(w2), 1, "e4m3")
    xs = mxq(f64(xT), 0, "e4m3")
    hs = relu(w1q[E].T @ xs) * (w3q[E].T @ xs)
    ys = w2q[E].T @ mxq(hs, 0, "e4m3")
    xq = mxq(f64(xT)[:, idx], 0, "e4m3")
    h = relu(by_expert(w1q, xq))
    h = h * by_expert(w3q, xq)
    y = by_expert(w2q, mxq(h, 0, "e4m3"))
    return ys + f64(gate[0]) * y[:, unstriped(pos1)] + f64(gate[1]) * y[:, unstriped(pos2)]

from contextlib import ExitStack

import concourse.mybir as mybir

K, T, E, C, H, N = 1024, 512, 4, 256, 512, 256

FLOPS = 2 * (E * C + T) * (2 * K * H + H * N)

F32 = mybir.dt.float32
BF16 = mybir.dt.bfloat16
U32 = mybir.dt.uint32
U16 = mybir.dt.uint16
U8 = mybir.dt.uint8
FP8X4 = mybir.dt.float8_e4m3fn_x4
MULT = mybir.AluOpType.mult
RELU = mybir.ActivationFunctionType.Relu

P = 128
J = 4
KC = K // (P * J)
G = 128
LOOKAHEAD = 8


def tile_moe_shr_glu_relu_kernel(tc, xT, w1, w3, w2, gate, offs, pos1, pos2, out):
    nc = tc.nc
    with ExitStack() as ctx:
        keep = ctx.enter_context(tc.tile_pool(name="keep", bufs=1))
        rawp = ctx.enter_context(tc.tile_pool(name="rawp", bufs=7))
        raw2p = ctx.enter_context(tc.tile_pool(name="raw2p", bufs=3))
        grp = ctx.enter_context(tc.tile_pool(name="grp", bufs=4))
        codep = ctx.enter_context(tc.tile_pool(name="codep", bufs=10))
        code2p = ctx.enter_context(tc.tile_pool(name="code2p", bufs=2))
        gxp = ctx.enter_context(tc.tile_pool(name="gxp", bufs=4))
        tokp = ctx.enter_context(tc.tile_pool(name="tokp", bufs=2))
        hp = ctx.enter_context(tc.tile_pool(name="hp", bufs=4))
        psa = ctx.enter_context(tc.psum_pool(name="psa", bufs=3))
        psb = ctx.enter_context(tc.psum_pool(name="psb", bufs=3))
        psy = ctx.enter_context(tc.psum_pool(name="psy", bufs=2))

        offs_t = keep.tile([P, E * C // 16], U16, name="offs_t")
        pos_t = [keep.tile([P, T // 16], U16, name="pos1_t"), keep.tile([P, T // 16], U16, name="pos2_t")]
        x_raw = [keep.tile([P, J, T], F32, name="x_raw%d" % c) for c in range(KC)]

        def load_x(c, u):
            src = xT[c * P * J : (c + 1) * P * J, :].rearrange("(p j) w -> p j w", j=J)
            nc.sync.dma_start(out=x_raw[c][:, 2 * u : 2 * u + 2, :], in_=src[:, 2 * u : 2 * u + 2, :])

        load_x(0, 0)
        nc.sync.dma_start(offs_t[:], offs)

        chunks = []
        for e in range(E + 1):
            chunks += [(e, "w1", 0), (e, "w1", 1), (e, "w3", 0), (e, "w3", 1), (e, "w2", 0)]
        raws = {}
        gates = [keep.tile([P, 2, T], F32, name="gate0"), keep.tile([P, 2, T], F32, name="gate1")]

        def load(q):
            e, which, c = chunks[q]
            if e == E and which == "w1" and c == 0:
                nc.sync.dma_start(pos_t[0][:], pos1)
                nc.sync.dma_start(pos_t[1][:], pos2)
                for r in range(2):
                    nc.sync.dma_start(out=gates[r][:], in_=gate[r].rearrange("(h p) t -> p h t", p=P))
            if which == "w2":
                t = raw2p.tile([P, J, N], F32, name="raw2")
                nc.sync.dma_start(out=t[:], in_=w2[e].rearrange("(p j) w -> p j w", j=J))
            else:
                w = w1 if which == "w1" else w3
                t = rawp.tile([P, J, H], F32, name="raw")
                nc.sync.dma_start(out=t[:], in_=w[e, c * P * J : (c + 1) * P * J, :].rearrange("(p j) w -> p j w", j=J))
            raws[q] = t

        load(0)
        load_x(0, 1)
        load(1)
        load_x(1, 0)
        load(2)
        load_x(1, 1)
        for q in range(3, LOOKAHEAD):
            load(q)

        x_pair = {}

        def pair_tokens(c, u):
            t = keep.tile([P, T, 2], BF16, name="x_pair%d%d" % (c, u), align_bytes=64)
            pairs = x_raw[c][:, 2 * u : 2 * u + 2, :].rearrange("p e n -> p n e")
            if u == 0:
                nc.vector.tensor_copy(out=t[:], in_=pairs)
            else:
                nc.scalar.copy(out=t[:], in_=pairs)
            x_pair[c, u] = t

        xs_codes = keep.tile([P, KC, T], U32, name="xs_codes", align_bytes=64)
        xs_scales = keep.tile([P, KC, T], U8, name="xs_scales", align_bytes=64)
        xs_grp = []
        for c in range(KC):
            t = keep.tile([P, T, J], BF16, name="xs_grp%d" % c, align_bytes=64)
            xs_grp.append(t)

        def group_shared_tokens(c, part):
            cols = slice(part * T // XPARTS, (part + 1) * T // XPARTS)
            nc.gpsimd.tensor_scalar(
                out=xs_grp[c][:, cols, :].rearrange("p (n i) j -> p n j i", i=4), in0=x_raw[c][:, :, cols].rearrange("p j (n i) -> p n j i", i=4),
                scalar1=1.0, scalar2=0.0, op0=MULT, op1=mybir.AluOpType.add,
            )

        gx = {}

        def gather(e, c, u):
            if e not in gx:
                gx[e] = gxp.tile([P, KC * C * J], BF16, name="gx", align_bytes=64)
            words = gx[e][:].bitcast(U32).rearrange("p (c n u) -> p c n u", c=KC, u=2)
            window = x_pair[c, u][:].rearrange("p n e -> p (n e)").bitcast(U32)
            nc.vector.tensor_copy(words[:, c, :, u], window.indirect(offs_t[:, e * C // 16 : (e + 1) * C // 16]))

        xcodes = {}

        def quantise_tokens(e):
            codes = tokp.tile([P, KC, C], U32, name="x_codes", align_bytes=64)
            scales = tokp.tile([P, KC, C], U8, name="x_scales", align_bytes=64)
            nc.vector.quantize_mx(
                out=codes[:].rearrange("p c n -> p (c n)").bitcast(FP8X4), scales=scales[:].rearrange("p c n -> p (c n)"), in_=gx[e][:]
            )
            xcodes[e] = (codes, scales)

        def quantise_shared_tokens(c):
            nc.vector.quantize_mx(out=xs_codes[:, c, :].bitcast(FP8X4), scales=xs_scales[:, c, :], in_=xs_grp[c][:].rearrange("p n j -> p (n j)"))
            xcodes[E] = (xs_codes, xs_scales)

        grouped = {}
        wcodes = {}

        def copy_weights(q):
            e, which, c = chunks[q]
            if which == "w2":
                g = grp.tile([P, N * J], BF16, name="grp2", align_bytes=64)
                dst = g[:].rearrange("p (n i j) -> p n j i", i=4, j=J)
                src = raws[q][:].rearrange("p j (n i) -> p n j i", i=4)
                count = N // 4
            else:
                g = grp.tile([P, H * J], BF16, name="grp", align_bytes=64)
                dst = g[:].rearrange("p (t m j) -> p m j t", t=J, j=J)
                src = raws[q][:].rearrange("p j (m t) -> p m j t", t=J)
                count = P
            share = VECTOR_SHARE[e][which, c] * count // 128
            if share < count:
                nc.scalar.copy(out=dst[:, share:], in_=src[:, share:])
            if share > 0:
                nc.vector.tensor_copy(out=dst[:, :share], in_=src[:, :share])
            grouped[q] = g

        def quantise_weights(q):
            e, which, c = chunks[q]
            if which == "w2":
                codes = code2p.tile([P, N], U32, name="w2_codes", align_bytes=64)
                scales = code2p.tile([P, N], U8, name="w2_scales", align_bytes=64)
            else:
                codes = codep.tile([P, H], U32, name="w_codes", align_bytes=64)
                scales = codep.tile([P, H], U8, name="w_scales", align_bytes=64)
            nc.vector.quantize_mx(out=codes[:].bitcast(FP8X4), scales=scales[:], in_=grouped[q][:])
            wcodes[e, which, c] = (codes, scales)

        def first_layer(e, which, g, pool):
            bank = pool.tile([P, J, G], F32, name="bank_" + which)
            xc, xsc = xcodes[e]
            for t in range(J):
                for c in range(KC):
                    wc, wsc = wcodes[e, which, c]
                    nc.tensor.matmul_mx(
                        out=bank[:, t, :],
                        lhsT=wc[:, t * P : (t + 1) * P].bitcast(FP8X4),
                        lhsT_scale=wsc[:, t * P : (t + 1) * P],
                        rhs=xc[:, c, g * G : (g + 1) * G].bitcast(FP8X4),
                        rhs_scale=xsc[:, c, g * G : (g + 1) * G],
                        start=(c == 0),
                        stop=(c == KC - 1),
                    )
            return bank

        relus = {}
        hgrp = {}
        hcodes = {}

        banks = {}

        def gate_matmuls(e, g):
            banks[e, "w1", g] = first_layer(e, "w1", g, psa)

        def up_matmuls(e, g):
            banks[e, "w3", g] = first_layer(e, "w3", g, psb)

        def gate_half(e, g):
            bank = banks[e, "w1", g]
            r = hp.tile([P, G, J], F32, name="relu_a")
            nc.scalar.activation(out=r[:], in_=bank[:].rearrange("p t n -> p n t"), func=RELU)
            relus[e, g] = r

        def up_half(e, g):
            bank = banks[e, "w3", g]
            if g % 2 == 0:
                hgrp[e, g // 2] = hp.tile([P, 2 * G, J], BF16, name="h_grp", align_bytes=64)
            h = hgrp[e, g // 2]
            nc.vector.tensor_tensor(
                out=h[:, (g % 2) * G : (g % 2 + 1) * G, :], in0=bank[:].rearrange("p t n -> p n t"), in1=relus[e, g][:], op=MULT
            )

        def quantise_hidden(e, pair, lo, hi):
            if (e, pair) not in hcodes:
                codes = hp.tile([P, 2 * G], U32, name="h_codes", align_bytes=64)
                scales = hp.tile([P, 2 * G], U8, name="h_scales", align_bytes=64)
                hcodes[e, pair] = (codes, scales)
            codes, scales = hcodes[e, pair]
            nc.vector.quantize_mx(
                out=codes[:, lo:hi].bitcast(FP8X4), scales=scales[:, lo:hi], in_=hgrp[e, pair][:, lo:hi, :].rearrange("p n j -> p (n j)")
            )

        ybank = {}

        def second_layer(e, pair, lo, hi):
            wc, wsc = wcodes[e, "w2", 0]
            if (e, pair) not in ybank:
                ybank[e, pair] = psy.tile([P, 2, 2 * G], F32, name="bank_y")
            bank = ybank[e, pair]
            codes, scales = hcodes[e, pair]
            for half in range(2):
                nc.tensor.matmul_mx(
                    out=bank[:, half, lo:hi],
                    lhsT=wc[:, half * P : (half + 1) * P].bitcast(FP8X4),
                    lhsT_scale=wsc[:, half * P : (half + 1) * P],
                    rhs=codes[:, lo:hi].bitcast(FP8X4),
                    rhs_scale=scales[:, lo:hi],
                    start=True,
                    stop=True,
                )

        y_sb = [keep.tile([P, E * C], F32, name="y_sb0"), keep.tile([P, E * C], F32, name="y_sb1")]

        def store_slots(e):
            for half in range(2):
                nc.scalar.copy(out=y_sb[half][:, e * C : (e + 1) * C], in_=ybank[e, 0][:, half, :])

        picked = [keep.tile([P, 2, T], F32, name="picked0"), keep.tile([P, 2, T], F32, name="picked1")]
        combined = keep.tile([P, 2, T], F32, name="combined")
        result = keep.tile([P, 2, T], F32, name="result")

        def pick(r, half):
            nc.vector.tensor_tensor(out=picked[r][:, half, :], in0=y_sb[half][:].indirect(pos_t[r][:]), in1=gates[r][:, half, :], op=MULT)

        def finish(pair):
            cols = slice(pair * 2 * G, (pair + 1) * 2 * G)
            nc.vector.tensor_add(out=result[:, :, cols], in0=ybank[E, pair][:], in1=combined[:, :, cols])
            for half in range(2):
                nc.sync.dma_start(out=out[half * P : (half + 1) * P, cols], in_=result[:, half, cols])

        def shared_group(g):
            up_half(E, g)

        def shared_out(g):
            lo, hi = (g % 2) * G, (g % 2 + 1) * G
            quantise_hidden(E, g // 2, lo, hi)
            second_layer(E, g // 2, lo, hi)
            if g % 2 == 1:
                finish(g // 2)

        def combine():
            nc.vector.tensor_add(out=combined[:], in0=picked[0][:], in1=picked[1][:])

        later = {}

        def at(step, rank, *call):
            later.setdefault(step, []).append((rank, len(later.get(step, [])), call))

        LQ, LR, LB, LH, LY = LAGS
        nq = len(chunks)
        for c in range(KC):
            for u in range(2):
                at(2 * c + u, -2, pair_tokens, c, u)
                for e in range(E):
                    at(2 * c + u + GATHER[e][0], GATHER[e][1], gather, e, c, u)
        for e in range(E):
            at(3 + GATHER[e][0] + (e > 0), GATHER[e][1], quantise_tokens, e)
        for c in range(KC):
            for part in range(XPARTS):
                at(XSTEP[c], 7, group_shared_tokens, c, part)
        for q in range(nq):
            e, which, c = chunks[q]
            groups = T // G if e == E else C // G
            if q + LOOKAHEAD < nq:
                at(q, -9, load, q + LOOKAHEAD)
            at(q, 1, copy_weights, q)
            at(q + LQ, 2, quantise_weights, q)
            if c == 1:
                base = q + LQ
                if e < E:
                    ready = 3 + GATHER[e][0] + (e > 0) + (GATHER[e][1] > 2.9)
                    base = max(base, ready)
                for g in range(groups):
                    if which == "w1":
                        at(base, 3, gate_matmuls, e, g) if e < E or g < 3 else at(base + LR, 4, gate_matmuls, e, g)
                        at(base + LR, 4, gate_half, e, g)
                    elif e < E:
                        at(base, 3, up_matmuls, e, g)
                        at(base + LB, 5, up_half, e, g)
                if which == "w3" and e < E:
                    at(base + LB + LH, RH, quantise_hidden, e, 0, 0, C)
                    at(base + LB + LH, RH, second_layer, e, 0, 0, C)
                    at(base + LB + LH + LY, RY, store_slots, e)
        at(XSTEP[0] + 5, 6, quantise_shared_tokens, 0)
        at(XSTEP[1] + 5, 6, quantise_shared_tokens, 1)
        s0 = 5 * E
        for r in range(2):
            for half in range(2):
                at(s0 + PICK[2 * r + half], 6, pick, r, half)
        at(s0 + PICK[4], 6, combine)
        n = nq + LQ
        for g in range(3):
            at(n - 1, 3, up_matmuls, E, g)
        at(n, 0, shared_group, 0)
        at(n, 0, shared_group, 1)
        at(n, 1, up_matmuls, E, 3)
        at(n, 1, shared_out, 0)
        at(n, 2, shared_group, 2)
        at(n, 3, shared_out, 1)
        at(n, 4, shared_group, 3)
        at(n, 5, shared_out, 2)
        at(n, 6, shared_out, 3)
        for step in sorted(later):
            for rank, order, call in sorted(later[step], key=lambda item: item[:2]):
                call[0](*call[1:])


XPARTS, XSTEP = 4, (11, 5)
GATHER = [[0, 4.5], [1, 1.5], [4, 4.5], [9, 6]]
LAGS = (1, 1, 1, 1, 1)
RH, RY, RG = (2, 1, 6)
PICK = (4, 2, 2, 3, 4)

VECTOR_SHARE = [{('w1', 0): 96, ('w1', 1): 0, ('w3', 0): 80, ('w3', 1): 0, ('w2', 0): 0}, {('w1', 0): 0, ('w1', 1): 0, ('w3', 0): 48, ('w3', 1): 0, ('w2', 0): 96}, {('w1', 0): 16, ('w1', 1): 0, ('w3', 0): 128, ('w3', 1): 0, ('w2', 0): 16}, {('w1', 0): 80, ('w1', 1): 96, ('w3', 0): 32, ('w3', 1): 80, ('w2', 0): 64}, {('w1', 0): 80, ('w1', 1): 48, ('w3', 0): 0, ('w3', 1): 32, ('w2', 0): 0}]
